import numpy as np
import ml_dtypes


def mxq(x, axis, fmt="e4m3"):
    dtype, down = {"e4m3": (ml_dtypes.float8_e4m3fn, 7), "e5m2": (ml_dtypes.float8_e5m2, 14)}[fmt]
    v = np.moveaxis(np.asarray(x, np.float32).astype(ml_dtypes.bfloat16).astype(np.float64), axis, -1)
    blocks = v.reshape(v.shape[:-1] + (-1, 32))
    amax = np.abs(blocks).max(-1, keepdims=True)
    byte = np.maximum(np.where(amax > 0, np.frexp(amax)[1] - 1 + 127, 0) - down, 1)
    scale = np.exp2(byte - 127.0)
    codes = (blocks / scale).astype(np.float32).astype(dtype).astype(np.float64)
    return np.moveaxis((codes * scale).reshape(v.shape), -1, axis)


WIDE = False


def mx_kscale(k):
    if not WIDE:
        return np.ones(k)
    levels = np.array([30, -30])
    if k % 512:
        return np.exp2(np.random.permutation(np.resize(levels, k // 32))).repeat(32)
    a = np.empty((k // 512, 16))
    for p in range(k // 512):
        a[p, :8] = np.random.permutation(np.resize(levels, 8))
        for g in range(8):
            far = levels[np.abs(levels - a[p, g]) >= 10]
            a[p, g + 8] = far[np.random.randint(len(far))]
    return np.exp2(a.ravel()).repeat(32)


def f64(x):
    return np.asarray(x).astype(np.float64)


E2M1 = np.array([0.0, 0.5, 1.0, 1.5, 2.0, 3.0, 4.0, 6.0, -0.0, -0.5, -1.0, -1.5, -2.0, -3.0, -4.0, -6.0])


def pack_weight(w, fmt):
    k, n = w.shape
    w = f64(np.asarray(w, np.float32).astype(ml_dtypes.bfloat16)).reshape(k // 32, 32, n)
    amax = np.abs(w).max(1)
    if fmt == "e4m3":
        byte = np.frexp(amax)[1] - 1 + 127 - 7
    else:
        mant, ex = np.frexp(amax / 6.0)
        byte = np.where(mant > 0.5, ex, ex - 1) + 127
    byte = np.clip(np.where(amax > 0, byte, 1), 1, 254)
    scaled = (w * np.exp2(127.0 - byte)[:, None, :]).reshape(k, n).astype(np.float32)
    by_word = np.ascontiguousarray(scaled.reshape(k // 512, 128, 4, n).transpose(0, 1, 3, 2))
    if fmt == "e4m3":
        words = by_word.astype(ml_dtypes.float8_e4m3fn).view(np.uint8)
    else:
        c = by_word.astype(ml_dtypes.float4_e2m1fn).view(np.uint8) & 0xF
        words = (c[..., 0::2] | (c[..., 1::2] << 4)).reshape(k // 512, 128, 2 * n)
    return np.ascontiguousarray(words), np.ascontiguousarray(byte.astype(np.uint8).reshape(k // 512, 16, n))


def unpack_weight(words, scales, fmt):
    g, _, n = scales.shape
    words = np.ascontiguousarray(words).reshape(g, 128, n, -1)
    if fmt == "e4m3":
        vals = words.view(ml_dtypes.float8_e4m3fn).astype(np.float64)
    else:
        nib = np.empty((g, 128, n, 4), np.uint8)
        nib[..., 0::2] = words & 0xF
        nib[..., 1::2] = words >> 4
        vals = E2M1[nib]
    vals = vals * np.repeat(np.exp2(scales.astype(np.float64) - 127.0), 8, axis=1)[..., None]
    return vals.transpose(0, 1, 3, 2).reshape(g * 512, n)


K, N, T, S = 512, 512, 1024, 1024


def setup_inputs():
    n = np.random.standard_normal
    ft = mx_kscale(T)
    fs = mx_kscale(S)
    sap = pack_weight(n((S, K)) / fs[:, None], "e4m3")
    sbp = pack_weight(n((S, N)) * fs[:, None], "e2m1")
    return {
        "xa": (n((K, T))).astype(np.float32),
        "xb": (n((N, T))).astype(np.float32),
        "ra": (np.random.uniform(0.5, 1.5, (1, T)) * ft).astype(np.float32),
        "rb": (np.random.uniform(0.5, 1.5, (1, T)) / ft).astype(np.float32),
        "sa_words": sap[0],
        "sa_scales": sap[1],
        "sb_words": sbp[0],
        "sb_scales": sbp[1],
    }


def reference(xa, xb, ra, rb, sa_words, sa_scales, sb_words, sb_scales):
    sau = unpack_weight(sa_words, sa_scales, "e4m3")
    sbu = unpack_weight(sb_words, sb_scales, "e2m1")
    da = (f64(xa) - np.mean(f64(xa), axis=1, keepdims=True)) * f64(ra)
    db = (f64(xb) - np.mean(f64(xb), axis=1, keepdims=True)) * f64(rb)
    ta = da.T
    tb = db.T
    taq = mxq(ta, 0, "e4m3")
    tbq = mxq(tb, 0, "e5m2")
    v = taq.T @ tbq + sau.T @ sbu
    y = 0.03 * v
    return y

@@ -1,0 +1,250 @@
+from contextlib import ExitStack
+
+import concourse.mybir as mybir
+from concourse.masks import make_identity
+
+K, N, T, S = 512, 512, 1024, 1024
+FLOPS = 2 * K * N * (T + S)
+
+F32 = mybir.dt.float32
+BF16 = mybir.dt.bfloat16
+I32 = mybir.dt.int32
+U32 = mybir.dt.uint32
+U8 = mybir.dt.uint8
+E4M3 = mybir.dt.float8_e4m3fn_x4
+E5M2 = mybir.dt.float8_e5m2_x4
+E2M1 = mybir.dt.float4_e2m1fn_x4
+ALU = mybir.AluOpType
+COPY = mybir.ActivationFunctionType.Copy
+
+P = 128
+PASSES = 2
+TILES = 4
+OUT_SCALE = 0.03
+VECTOR_SUMS = (0, 3)
+WORDS_AFTER = 5
+SCALES_AFTER = 2
+
+
+def tile_mix_covariances_of_two_stores_kernel(tc, xa, xb, ra, rb, sa_words, sa_scales, sb_words, sb_scales, out):
+    nc = tc.nc
+    steps = 2 * TILES
+    last = steps - 1
+
+    with ExitStack() as ctx:
+        keep = ctx.enter_context(tc.tile_pool(name="keep", bufs=1))
+        rows = ctx.enter_context(tc.tile_pool(name="rows", bufs=steps))
+        psum = ctx.enter_context(tc.psum_pool(name="psum", bufs=1))
+        ctx.enter_context(tc.manual_schedule())
+
+        def bank(tag, shape):
+            return psum.tile(shape, F32, name="bank", tag=tag)
+
+        r_cols = []
+        for name, r in (("rb_cols", rb), ("ra_cols", ra)):
+            cols = keep.tile([P, PASSES, 4], F32, name=name)
+            nc.scalar.dma_start(out=cols[:], in_=r[0, :].rearrange("(c p j) -> p c j", c=PASSES, j=4))
+            r_cols.append(cols)
+
+        sa_codes = keep.tile([P, PASSES, 4 * K], U8, align_bytes=64)
+        sb_codes = keep.tile([P, PASSES, 2 * N], U8, align_bytes=64)
+        sa_plane = keep.tile([P, PASSES, K], U8, align_bytes=64)
+        sb_plane = keep.tile([P, PASSES, N], U8, align_bytes=64)
+        nc.vector.memset(sb_plane[:].bitcast(I32), 0)
+        nc.vector.memset(sa_plane[:].bitcast(I32), 0)
+        x_rows = []
+        for i in range(steps):
+            src = xb if i < TILES else xa
+            x_tile = rows.tile([P, T], F32, name="x_tile")
+            row0 = (i % TILES) * P
+            nc.sync.dma_start(out=x_tile[:], in_=src[row0 : row0 + P, :])
+            x_rows.append(x_tile)
+            if i == WORDS_AFTER:
+                nc.sync.dma_start(out=sb_codes[:].bitcast(I32), in_=sb_words.rearrange("z p b -> p z b").bitcast(I32))
+                nc.sync.dma_start(
+                    out=sa_codes[:].bitcast(I32), in_=sa_words.rearrange("z p c r -> p z (c r)").bitcast(I32)
+                )
+            if SCALES_AFTER <= i < SCALES_AFTER + 4:
+                q = i - SCALES_AFTER
+                for plane, scales in ((sb_plane, sb_scales), (sa_plane, sa_scales)):
+                    nc.sync.dma_start(
+                        out=plane[32 * q : 32 * q + 4, :, :].bitcast(I32),
+                        in_=scales[:, 4 * q : 4 * q + 4, :].rearrange("z q c -> q z c").bitcast(I32),
+                    )
+
+        ident = keep.tile([P, P], F32)
+        make_identity(nc, ident[:])
+
+        ta_codes = keep.tile([P, PASSES, K], U32, align_bytes=64)
+        tb_codes = keep.tile([P, PASSES, N], U32, align_bytes=64)
+        ta_plane = keep.tile([P, PASSES, K], U8, align_bytes=64)
+        tb_plane = keep.tile([P, PASSES, N], U8, align_bytes=64)
+
+        r_banks = {}
+        neg_mean = {}
+        totals = {}
+        centred = {}
+        turned = {}
+        grouped = {}
+        acc = {}
+
+        def spread_weights(which, u):
+            tag = ("acc%d" % (2 + u)) if which == 0 else ("ra%d" % u)
+            spread = bank(tag, [P, 2, PASSES, P])
+            for e in range(2):
+                for c in range(PASSES):
+                    j = 2 * u + e
+                    nc.tensor.transpose(
+                        spread[:, e, c, :], r_cols[which][:, c, j : j + 1].to_broadcast([P, P]), ident[:]
+                    )
+            r_banks[which, u] = spread
+
+        def row_mean(i):
+            mean = rows.tile([P, 1], F32, name="mean")
+            if i in VECTOR_SUMS:
+                total = rows.tile([P, 1], F32, name="total", bufs=len(VECTOR_SUMS))
+                folded = rows.tile([P, T // 2], F32, name="folded", bufs=len(VECTOR_SUMS))
+                nc.vector.scalar_tensor_tensor(
+                    out=folded[:], in0=x_rows[i][:, : T // 2], scalar=1.0, in1=x_rows[i][:, T // 2 :],
+                    op0=ALU.mult, op1=ALU.add, accum_out=total[:],
+                )
+                totals[i] = total
+            else:
+                scaled = rows.tile([P, T], F32, name="scaled")
+                nc.scalar.activation(out=scaled[:], in_=x_rows[i][:], func=COPY, scale=-1.0 / T, accum_out=mean[:])
+            neg_mean[i] = mean
+
+        def finish_mean(i):
+            if i in VECTOR_SUMS:
+                nc.vector.tensor_scalar(out=neg_mean[i][:], in0=totals[i][:], scalar1=-1.0 / T, scalar2=None, op0=ALU.mult)
+
+        def centre(i, u, passes):
+            which = i // TILES
+            pairs = slice(passes.start * P, passes.stop * P)
+            x_pairs = x_rows[i][:].rearrange("p (n j) -> p n j", j=4)[:, pairs, 2 * u : 2 * u + 2]
+            r_pairs = r_banks[which, u][:].rearrange("p e c n -> p (c n) e")[:, pairs, :]
+            nc.vector.scalar_tensor_tensor(
+                out=centred[i][:].rearrange("p (u n e) -> p u n e", u=2, e=2)[:, u, pairs, :],
+                in0=x_pairs, scalar=neg_mean[i][:], in1=r_pairs, op0=ALU.add, op1=ALU.mult,
+            )
+
+        def turn(i, u, c, dst):
+            words = centred[i][:].bitcast(F32)
+            w0 = (u * PASSES + c) * P
+            nc.tensor.transpose(dst, words[:, w0 : w0 + P], ident[:])
+
+        def quantise(i, c):
+            cols = slice((i % TILES) * P, (i % TILES + 1) * P)
+            codes, plane, fmt = (tb_codes, tb_plane, E5M2) if i < TILES else (ta_codes, ta_plane, E4M3)
+            nc.vector.quantize_mx(
+                out=codes[:, c, cols].bitcast(fmt), scales=plane[:, c, cols],
+                in_=grouped[i][:, c * 4 * P : (c + 1) * 4 * P],
+            )
+
+        def stored_passes(m):
+            acc[m] = bank("acc%d" % m, [P, N])
+            for z in range(PASSES):
+                nc.tensor.matmul_mx(
+                    out=acc[m][:],
+                    lhsT=sa_codes[:, z, 4 * P * m : 4 * P * (m + 1)].bitcast(E4M3),
+                    lhsT_scale=sa_plane[:, z, P * m : P * (m + 1)],
+                    rhs=sb_codes[:, z, :].bitcast(E2M1),
+                    rhs_scale=sb_plane[:, z, :],
+                    start=(z == 0), stop=False,
+                )
+
+        def fresh_pass(m, c):
+            nc.tensor.matmul_mx(
+                out=acc[m][:],
+                lhsT=ta_codes[:, c, P * m : P * (m + 1)].bitcast(E4M3),
+                lhsT_scale=ta_plane[:, c, P * m : P * (m + 1)],
+                rhs=tb_codes[:, c, :].bitcast(E5M2),
+                rhs_scale=tb_plane[:, c, :],
+                start=False, stop=(c == PASSES - 1),
+            )
+
+        def store(m, on_vector):
+            result = rows.tile([P, N], F32, name="result", bufs=TILES)
+            if on_vector:
+                nc.vector.tensor_scalar(out=result[:], in0=acc[m][:], scalar1=OUT_SCALE, scalar2=None, op0=ALU.mult)
+            else:
+                nc.scalar.activation(out=result[:], in_=acc[m][:], func=COPY, scale=OUT_SCALE)
+            nc.sync.dma_start(out=out[m * P : (m + 1) * P, :], in_=result[:])
+
+        def copy_out(i):
+            grouped[i] = rows.tile([P, T], BF16, name="grouped", align_bytes=64)
+            nc.scalar.copy(
+                out=grouped[i][:].bitcast(F32).rearrange("p (c k u) -> p c k u", c=PASSES, u=2),
+                in_=turned[i][:].rearrange("p c u k -> p c k u"),
+            )
+
+        def turn_tag(i):
+            return ("acc%d" % i) if i < 2 else ("turn%d" % (i % 2))
+
+        both = range(0, PASSES)
+        spread_weights(0, 0)
+        spread_weights(0, 1)
+        row_mean(0)
+        finish_mean(0)
+        row_mean(1)
+        for s in range(last):
+            if s > 0:
+                row_mean(s + 1)
+            centred[s] = rows.tile([P, T], BF16, name="centred")
+            centre(s, 0, both)
+            finish_mean(s + 1)
+            centre(s, 1, both)
+            if s > 0:
+                copy_out(s - 1)
+            turned[s] = bank(turn_tag(s), [P, PASSES, 2, P])
+            for u in range(2):
+                for c in range(PASSES):
+                    turn(s, u, c, turned[s][:, c, u, :])
+            if s < 2:
+                spread_weights(1, s)
+            if s in (3, 4):
+                stored_passes(2 * (s - 3))
+                stored_passes(2 * (s - 3) + 1)
+            if s >= 2:
+                for c in range(PASSES):
+                    quantise(s - 2, c)
+            if s - 2 >= TILES:
+                for c in range(PASSES):
+                    fresh_pass(s - 2 - TILES, c)
+
+        centred[last] = rows.tile([P, T], BF16, name="centred")
+        for c in range(PASSES):
+            for u in range(2):
+                centre(last, u, range(c, c + 1))
+        copy_out(last - 1)
+        halves = []
+        for c in range(PASSES):
+            half = bank(turn_tag(last + c), [P, 2, P])
+            for u in range(2):
+                turn(last, u, c, half[:, u, :])
+            halves.append(half)
+        grouped[last] = rows.tile([P, T], BF16, name="grouped", align_bytes=64)
+
+        def copy_half(c):
+            nc.scalar.copy(
+                out=grouped[last][:].bitcast(F32).rearrange("p (c k u) -> p c k u", c=PASSES, u=2)[:, c, :, :],
+                in_=halves[c][:].rearrange("p u k -> p k u"),
+            )
+
+        for c in range(PASSES):
+            quantise(last - 2, c)
+        for c in range(PASSES):
+            fresh_pass(1, c)
+        store(0, False)
+        copy_half(0)
+        for c in range(PASSES):
+            quantise(last - 1, c)
+        for c in range(PASSES):
+            fresh_pass(2, c)
+        copy_half(1)
+        for c in range(PASSES):
+            quantise(last, c)
+            fresh_pass(3, c)
+        store(1, False)
+        store(2, True)
+        store(3, False)

@@ -21,9 +21,8 @@ P = 128
 PASSES = 2
 TILES = 4
 OUT_SCALE = 0.03
-VECTOR_SUMS = (0, 3)
-WORDS_AFTER = 5
-SCALES_AFTER = 2
+VECTOR_SUM = 4
+FIRST_STORED_STEP = 3
 
 
 def tile_mix_covariances_of_two_stores_kernel(tc, xa, xb, ra, rb, sa_words, sa_scales, sb_words, sb_scales, out):
@@ -40,49 +39,68 @@ def tile_mix_covariances_of_two_stores_kernel(tc, xa, xb, ra, rb, sa_words, sa_s
         def bank(tag, shape):
             return psum.tile(shape, F32, name="bank", tag=tag)
 
-        r_cols = []
-        for name, r in (("rb_cols", rb), ("ra_cols", ra)):
-            cols = keep.tile([P, PASSES, 4], F32, name=name)
-            nc.scalar.dma_start(out=cols[:], in_=r[0, :].rearrange("(c p j) -> p c j", c=PASSES, j=4))
-            r_cols.append(cols)
-
-        sa_codes = keep.tile([P, PASSES, 4 * K], U8, align_bytes=64)
+        rb_cols = keep.tile([P, PASSES, 4], F32)
+        ra_cols = keep.tile([P, PASSES, 4], F32)
+        r_cols = (rb_cols, ra_cols)
+        sa_codes = keep.tile([P, 2, PASSES, 2 * K], U8, align_bytes=64)
         sb_codes = keep.tile([P, PASSES, 2 * N], U8, align_bytes=64)
         sa_plane = keep.tile([P, PASSES, K], U8, align_bytes=64)
         sb_plane = keep.tile([P, PASSES, N], U8, align_bytes=64)
         nc.vector.memset(sb_plane[:].bitcast(I32), 0)
         nc.vector.memset(sa_plane[:].bitcast(I32), 0)
         x_rows = []
-        for i in range(steps):
+
+        def load_weights(engine, cols, r):
+            engine.dma_start(out=cols[:], in_=r[0, :].rearrange("(c p j) -> p c j", c=PASSES, j=4))
+
+        def load_rows(i, pieces=1):
             src = xb if i < TILES else xa
             x_tile = rows.tile([P, T], F32, name="x_tile")
             row0 = (i % TILES) * P
-            nc.sync.dma_start(out=x_tile[:], in_=src[row0 : row0 + P, :])
+            width = T // pieces
+            for t0 in range(0, T, width):
+                nc.sync.dma_start(out=x_tile[:, t0 : t0 + width], in_=src[row0 : row0 + P, t0 : t0 + width])
             x_rows.append(x_tile)
-            if i == WORDS_AFTER:
-                nc.sync.dma_start(out=sb_codes[:].bitcast(I32), in_=sb_words.rearrange("z p b -> p z b").bitcast(I32))
+
+        def load_scales(plane, scales):
+            for q in range(4):
                 nc.sync.dma_start(
-                    out=sa_codes[:].bitcast(I32), in_=sa_words.rearrange("z p c r -> p z (c r)").bitcast(I32)
+                    out=plane[32 * q : 32 * q + 4, :, :].bitcast(I32),
+                    in_=scales[:, 4 * q : 4 * q + 4, :].rearrange("z q c -> q z c").bitcast(I32),
                 )
-            if SCALES_AFTER <= i < SCALES_AFTER + 4:
-                q = i - SCALES_AFTER
-                for plane, scales in ((sb_plane, sb_scales), (sa_plane, sa_scales)):
-                    nc.sync.dma_start(
-                        out=plane[32 * q : 32 * q + 4, :, :].bitcast(I32),
-                        in_=scales[:, 4 * q : 4 * q + 4, :].rearrange("z q c -> q z c").bitcast(I32),
-                    )
+
+        def load_sa_words(h):
+            nc.sync.dma_start(
+                out=sa_codes[:, h, :, :].bitcast(I32),
+                in_=sa_words[:, :, h * (K // 2) : (h + 1) * (K // 2), :].rearrange("z p c r -> p z (c r)").bitcast(I32),
+            )
+
+        load_weights(nc.scalar, rb_cols, rb)
+        load_rows(0, pieces=2)
+        load_rows(1)
+        load_scales(sb_plane, sb_scales)
+        load_rows(2)
+        load_weights(nc.sync, ra_cols, ra)
+        load_rows(3)
+        load_scales(sa_plane, sa_scales)
+        load_rows(4)
+        nc.sync.dma_start(out=sb_codes[:].bitcast(I32), in_=sb_words.rearrange("z p b -> p z b").bitcast(I32))
+        load_sa_words(0)
+        load_rows(5)
+        load_rows(6)
+        load_sa_words(1)
+        load_rows(7)
 
         ident = keep.tile([P, P], F32)
         make_identity(nc, ident[:])
 
-        ta_codes = keep.tile([P, PASSES, K], U32, align_bytes=64)
+        ta_codes = keep.tile([P, TILES * PASSES * P], U32, align_bytes=64)
         tb_codes = keep.tile([P, PASSES, N], U32, align_bytes=64)
-        ta_plane = keep.tile([P, PASSES, K], U8, align_bytes=64)
+        ta_plane = keep.tile([P, TILES * PASSES * P], U8, align_bytes=64)
         tb_plane = keep.tile([P, PASSES, N], U8, align_bytes=64)
 
         r_banks = {}
         neg_mean = {}
-        totals = {}
         centred = {}
         turned = {}
         grouped = {}
@@ -99,24 +117,26 @@ def tile_mix_covariances_of_two_stores_kernel(tc, xa, xb, ra, rb, sa_words, sa_s
                     )
             r_banks[which, u] = spread
 
-        def row_mean(i):
-            mean = rows.tile([P, 1], F32, name="mean")
-            if i in VECTOR_SUMS:
-                total = rows.tile([P, 1], F32, name="total", bufs=len(VECTOR_SUMS))
-                folded = rows.tile([P, T // 2], F32, name="folded", bufs=len(VECTOR_SUMS))
-                nc.vector.scalar_tensor_tensor(
-                    out=folded[:], in0=x_rows[i][:, : T // 2], scalar=1.0, in1=x_rows[i][:, T // 2 :],
-                    op0=ALU.mult, op1=ALU.add, accum_out=total[:],
-                )
-                totals[i] = total
-            else:
-                scaled = rows.tile([P, T], F32, name="scaled")
-                nc.scalar.activation(out=scaled[:], in_=x_rows[i][:], func=COPY, scale=-1.0 / T, accum_out=mean[:])
-            neg_mean[i] = mean
+        def scalar_mean(i, width):
+            part = rows.tile([P, 1], F32, name="part")
+            scaled = rows.tile([P, width], F32, name="scaled")
+            nc.scalar.activation(out=scaled[:], in_=x_rows[i][:, :width], func=COPY, scale=-1.0 / T, accum_out=part[:])
+            return part
 
-        def finish_mean(i):
-            if i in VECTOR_SUMS:
-                nc.vector.tensor_scalar(out=neg_mean[i][:], in0=totals[i][:], scalar1=-1.0 / T, scalar2=None, op0=ALU.mult)
+        def vector_total(i, t0):
+            half = (T - t0) // 2
+            total = rows.tile([P, 1], F32, name="total", bufs=2)
+            folded = rows.tile([P, half], F32, name="folded", bufs=2)
+            nc.vector.scalar_tensor_tensor(
+                out=folded[:], in0=x_rows[i][:, t0 : t0 + half], scalar=1.0, in1=x_rows[i][:, t0 + half :],
+                op0=ALU.mult, op1=ALU.add, accum_out=total[:],
+            )
+            return total
+
+        def vector_mean(total, rest):
+            mean = rows.tile([P, 1], F32, name="mean", bufs=2)
+            nc.vector.tensor_scalar(out=mean[:], in0=total[:], scalar1=-1.0 / T, scalar2=rest, op0=ALU.mult, op1=ALU.add)
+            return mean
 
         def centre(i, u, passes):
             which = i // TILES
@@ -133,12 +153,19 @@ def tile_mix_covariances_of_two_stores_kernel(tc, xa, xb, ra, rb, sa_words, sa_s
             w0 = (u * PASSES + c) * P
             nc.tensor.transpose(dst, words[:, w0 : w0 + P], ident[:])
 
-        def quantise(i, c):
-            cols = slice((i % TILES) * P, (i % TILES + 1) * P)
-            codes, plane, fmt = (tb_codes, tb_plane, E5M2) if i < TILES else (ta_codes, ta_plane, E4M3)
+        def quantise_b(pair):
+            cols = slice(pair * 2 * P, (pair + 1) * 2 * P)
+            for c in range(PASSES):
+                nc.vector.quantize_mx(
+                    out=tb_codes[:, c, cols].bitcast(E5M2), scales=tb_plane[:, c, cols],
+                    in_=grouped[2 * pair][:, c * 8 * P : (c + 1) * 8 * P],
+                )
+
+        def quantise_a(m, passes):
+            cols = slice((m * PASSES + passes.start) * P, (m * PASSES + passes.stop) * P)
             nc.vector.quantize_mx(
-                out=codes[:, c, cols].bitcast(fmt), scales=plane[:, c, cols],
-                in_=grouped[i][:, c * 4 * P : (c + 1) * 4 * P],
+                out=ta_codes[:, cols].bitcast(E4M3), scales=ta_plane[:, cols],
+                in_=grouped[TILES + m][:, passes.start * 4 * P : passes.stop * 4 * P],
             )
 
         def stored_passes(m):
@@ -146,7 +173,7 @@ def tile_mix_covariances_of_two_stores_kernel(tc, xa, xb, ra, rb, sa_words, sa_s
             for z in range(PASSES):
                 nc.tensor.matmul_mx(
                     out=acc[m][:],
-                    lhsT=sa_codes[:, z, 4 * P * m : 4 * P * (m + 1)].bitcast(E4M3),
+                    lhsT=sa_codes[:, m // 2, z, 4 * P * (m % 2) : 4 * P * (m % 2 + 1)].bitcast(E4M3),
                     lhsT_scale=sa_plane[:, z, P * m : P * (m + 1)],
                     rhs=sb_codes[:, z, :].bitcast(E2M1),
                     rhs_scale=sb_plane[:, z, :],
@@ -154,97 +181,105 @@ def tile_mix_covariances_of_two_stores_kernel(tc, xa, xb, ra, rb, sa_words, sa_s
                 )
 
         def fresh_pass(m, c):
+            cols = slice((m * PASSES + c) * P, (m * PASSES + c + 1) * P)
             nc.tensor.matmul_mx(
                 out=acc[m][:],
-                lhsT=ta_codes[:, c, P * m : P * (m + 1)].bitcast(E4M3),
-                lhsT_scale=ta_plane[:, c, P * m : P * (m + 1)],
+                lhsT=ta_codes[:, cols].bitcast(E4M3),
+                lhsT_scale=ta_plane[:, cols],
                 rhs=tb_codes[:, c, :].bitcast(E5M2),
                 rhs_scale=tb_plane[:, c, :],
                 start=False, stop=(c == PASSES - 1),
             )
 
-        def store(m, on_vector):
-            result = rows.tile([P, N], F32, name="result", bufs=TILES)
-            if on_vector:
-                nc.vector.tensor_scalar(out=result[:], in0=acc[m][:], scalar1=OUT_SCALE, scalar2=None, op0=ALU.mult)
-            else:
-                nc.scalar.activation(out=result[:], in_=acc[m][:], func=COPY, scale=OUT_SCALE)
+        def store(m):
+            result = rows.tile([P, N], F32, name="result", bufs=TILES - 1)
+            nc.scalar.activation(out=result[:], in_=acc[m][:], func=COPY, scale=OUT_SCALE)
             nc.sync.dma_start(out=out[m * P : (m + 1) * P, :], in_=result[:])
 
-        def copy_out(i):
-            grouped[i] = rows.tile([P, T], BF16, name="grouped", align_bytes=64)
-            nc.scalar.copy(
-                out=grouped[i][:].bitcast(F32).rearrange("p (c k u) -> p c k u", c=PASSES, u=2),
-                in_=turned[i][:].rearrange("p c u k -> p c k u"),
-            )
+        def store_last_half(h):
+            m = TILES - 1
+            cols = slice(h * (N // 2), (h + 1) * (N // 2))
+            result_half = rows.tile([P, N // 2], F32, name="result_half", bufs=2)
+            nc.vector.tensor_scalar(out=result_half[:], in0=acc[m][:, cols], scalar1=OUT_SCALE, scalar2=None, op0=ALU.mult)
+            nc.sync.dma_start(out=out[m * P : (m + 1) * P, cols], in_=result_half[:])
 
-        def turn_tag(i):
-            return ("acc%d" % i) if i < 2 else ("turn%d" % (i % 2))
+        def copy_out(i):
+            if i >= TILES:
+                grouped[i] = rows.tile([P, T], BF16, name="grouped_a", bufs=TILES, align_bytes=64)
+                dst = grouped[i][:].bitcast(F32).rearrange("p (c k u) -> p c k u", c=PASSES, u=2)
+            else:
+                if i % 2 == 0:
+                    grouped[i] = rows.tile([P, 2 * T], BF16, name="grouped_b", bufs=2, align_bytes=64)
+                both_tiles = grouped[i - i % 2][:].bitcast(F32).rearrange("p (c i k u) -> p c i k u", c=PASSES, i=2, u=2)
+                dst = both_tiles[:, :, i % 2, :, :]
+            nc.scalar.copy(out=dst, in_=turned[i][:].rearrange("p c u k -> p c k u"))
 
         both = range(0, PASSES)
         spread_weights(0, 0)
         spread_weights(0, 1)
-        row_mean(0)
-        finish_mean(0)
-        row_mean(1)
+        first_half = scalar_mean(0, T // 2)
+        neg_mean[0] = vector_mean(vector_total(0, T // 2), first_half[:])
+        neg_mean[1] = scalar_mean(1, T)
         for s in range(last):
-            if s > 0:
-                row_mean(s + 1)
             centred[s] = rows.tile([P, T], BF16, name="centred")
-            centre(s, 0, both)
-            finish_mean(s + 1)
-            centre(s, 1, both)
+            if s + 1 == VECTOR_SUM:
+                total = vector_total(s + 1, 0)
+                centre(s, 0, both)
+                neg_mean[s + 1] = vector_mean(total, 0.0)
+                centre(s, 1, both)
+            else:
+                if s > 0:
+                    neg_mean[s + 1] = scalar_mean(s + 1, T)
+                centre(s, 0, both)
+                centre(s, 1, both)
             if s > 0:
                 copy_out(s - 1)
-            turned[s] = bank(turn_tag(s), [P, PASSES, 2, P])
+            if s >= FIRST_STORED_STEP:
+                stored_passes(s - FIRST_STORED_STEP)
+            turned[s] = bank("turn%d" % (s % 2), [P, PASSES, 2, P])
             for u in range(2):
                 for c in range(PASSES):
                     turn(s, u, c, turned[s][:, c, u, :])
-            if s < 2:
-                spread_weights(1, s)
-            if s in (3, 4):
-                stored_passes(2 * (s - 3))
-                stored_passes(2 * (s - 3) + 1)
-            if s >= 2:
+            if s in (1, 2):
+                spread_weights(1, s - 1)
+            if s in (3, 5):
+                quantise_b((s - 3) // 2)
+            if s == 6:
+                quantise_a(0, both)
                 for c in range(PASSES):
-                    quantise(s - 2, c)
-            if s - 2 >= TILES:
-                for c in range(PASSES):
-                    fresh_pass(s - 2 - TILES, c)
+                    fresh_pass(0, c)
 
         centred[last] = rows.tile([P, T], BF16, name="centred")
-        for c in range(PASSES):
-            for u in range(2):
-                centre(last, u, range(c, c + 1))
-        copy_out(last - 1)
-        halves = []
-        for c in range(PASSES):
-            half = bank(turn_tag(last + c), [P, 2, P])
+        grouped[last] = rows.tile([P, T], BF16, name="grouped_a", bufs=TILES, align_bytes=64)
+        last_words = grouped[last][:].bitcast(F32).rearrange("p (c k u) -> p c k u", c=PASSES, u=2)
+
+        def turn_last(c):
+            half = bank("turn%d" % ((last + c) % 2), [P, 2, P])
             for u in range(2):
                 turn(last, u, c, half[:, u, :])
-            halves.append(half)
-        grouped[last] = rows.tile([P, T], BF16, name="grouped", align_bytes=64)
+            return half[:].rearrange("p u k -> p k u")
 
-        def copy_half(c):
-            nc.scalar.copy(
-                out=grouped[last][:].bitcast(F32).rearrange("p (c k u) -> p c k u", c=PASSES, u=2)[:, c, :, :],
-                in_=halves[c][:].rearrange("p u k -> p k u"),
-            )
-
-        for c in range(PASSES):
-            quantise(last - 2, c)
+        for u in range(2):
+            centre(last, u, range(0, 1))
+        copy_out(last - 1)
+        quantise_a(1, both)
+        half0 = turn_last(0)
         for c in range(PASSES):
             fresh_pass(1, c)
-        store(0, False)
-        copy_half(0)
-        for c in range(PASSES):
-            quantise(last - 1, c)
+        for u in range(2):
+            centre(last, u, range(1, 2))
+        store(0)
+        quantise_a(2, both)
+        half1 = turn_last(1)
+        nc.scalar.copy(out=last_words[:, 0, :, :], in_=half0)
         for c in range(PASSES):
             fresh_pass(2, c)
-        copy_half(1)
-        for c in range(PASSES):
-            quantise(last, c)
-            fresh_pass(3, c)
-        store(1, False)
-        store(2, True)
-        store(3, False)
+        quantise_a(3, range(0, 1))
+        fresh_pass(3, 0)
+        nc.vector.tensor_copy(out=last_words[:, 1, :, :], in_=half1)
+        store(1)
+        quantise_a(3, range(1, 2))
+        fresh_pass(3, 1)
+        store(2)
+        store_last_half(0)
+        store_last_half(1)

@@ -42,12 +42,14 @@ def tile_mix_covariances_of_two_stores_kernel(tc, xa, xb, ra, rb, sa_words, sa_s
         rb_cols = keep.tile([P, PASSES, 4], F32)
         ra_cols = keep.tile([P, PASSES, 4], F32)
         r_cols = (rb_cols, ra_cols)
-        sa_codes = keep.tile([P, 2, PASSES, 2 * K], U8, align_bytes=64)
-        sb_codes = keep.tile([P, PASSES, 2 * N], U8, align_bytes=64)
+        sa_codes = [keep.tile([P, 4 * K], U8, name="sa_codes%d" % z, align_bytes=64) for z in range(PASSES)]
+        sb_codes = [keep.tile([P, 2 * N], U8, name="sb_codes%d" % z, align_bytes=64) for z in range(PASSES)]
         sa_plane = keep.tile([P, PASSES, K], U8, align_bytes=64)
         sb_plane = keep.tile([P, PASSES, N], U8, align_bytes=64)
-        nc.vector.memset(sb_plane[:].bitcast(I32), 0)
-        nc.vector.memset(sa_plane[:].bitcast(I32), 0)
+        ident = keep.tile([P, P], F32)
+        make_identity(nc, ident[:])
+        nc.gpsimd.memset(sb_plane[:].bitcast(I32), 0)
+        nc.gpsimd.memset(sa_plane[:].bitcast(I32), 0)
         x_rows = []
 
         def load_weights(engine, cols, r):
@@ -69,10 +71,10 @@ def tile_mix_covariances_of_two_stores_kernel(tc, xa, xb, ra, rb, sa_words, sa_s
                     in_=scales[:, 4 * q : 4 * q + 4, :].rearrange("z q c -> q z c").bitcast(I32),
                 )
 
-        def load_sa_words(h):
+        def load_words(z):
+            nc.sync.dma_start(out=sb_codes[z][:].bitcast(I32), in_=sb_words[z, :, :].bitcast(I32))
             nc.sync.dma_start(
-                out=sa_codes[:, h, :, :].bitcast(I32),
-                in_=sa_words[:, :, h * (K // 2) : (h + 1) * (K // 2), :].rearrange("z p c r -> p z (c r)").bitcast(I32),
+                out=sa_codes[z][:].bitcast(I32), in_=sa_words[z, :, :, :].rearrange("p c r -> p (c r)").bitcast(I32)
             )
 
         load_weights(nc.scalar, rb_cols, rb)
@@ -84,15 +86,11 @@ def tile_mix_covariances_of_two_stores_kernel(tc, xa, xb, ra, rb, sa_words, sa_s
         load_rows(3)
         load_scales(sa_plane, sa_scales)
         load_rows(4)
-        nc.sync.dma_start(out=sb_codes[:].bitcast(I32), in_=sb_words.rearrange("z p b -> p z b").bitcast(I32))
-        load_sa_words(0)
+        load_words(0)
         load_rows(5)
         load_rows(6)
-        load_sa_words(1)
+        load_words(1)
         load_rows(7)
-
-        ident = keep.tile([P, P], F32)
-        make_identity(nc, ident[:])
 
         ta_codes = keep.tile([P, TILES * PASSES * P], U32, align_bytes=64)
         tb_codes = keep.tile([P, PASSES, N], U32, align_bytes=64)
@@ -168,17 +166,17 @@ def tile_mix_covariances_of_two_stores_kernel(tc, xa, xb, ra, rb, sa_words, sa_s
                 in_=grouped[TILES + m][:, passes.start * 4 * P : passes.stop * 4 * P],
             )
 
-        def stored_passes(m):
-            acc[m] = bank("acc%d" % m, [P, N])
-            for z in range(PASSES):
-                nc.tensor.matmul_mx(
-                    out=acc[m][:],
-                    lhsT=sa_codes[:, m // 2, z, 4 * P * (m % 2) : 4 * P * (m % 2 + 1)].bitcast(E4M3),
-                    lhsT_scale=sa_plane[:, z, P * m : P * (m + 1)],
-                    rhs=sb_codes[:, z, :].bitcast(E2M1),
-                    rhs_scale=sb_plane[:, z, :],
-                    start=(z == 0), stop=False,
-                )
+        def stored_pass(m, z):
+            if z == 0:
+                acc[m] = bank("acc%d" % m, [P, N])
+            nc.tensor.matmul_mx(
+                out=acc[m][:],
+                lhsT=sa_codes[z][:, 4 * P * m : 4 * P * (m + 1)].bitcast(E4M3),
+                lhsT_scale=sa_plane[:, z, P * m : P * (m + 1)],
+                rhs=sb_codes[z][:].bitcast(E2M1),
+                rhs_scale=sb_plane[:, z, :],
+                start=(z == 0), stop=False,
+            )
 
         def fresh_pass(m, c):
             cols = slice((m * PASSES + c) * P, (m * PASSES + c + 1) * P)
@@ -235,7 +233,9 @@ def tile_mix_covariances_of_two_stores_kernel(tc, xa, xb, ra, rb, sa_words, sa_s
             if s > 0:
                 copy_out(s - 1)
             if s >= FIRST_STORED_STEP:
-                stored_passes(s - FIRST_STORED_STEP)
+                z, pair = divmod(s - FIRST_STORED_STEP, 2)
+                stored_pass(2 * pair, z)
+                stored_pass(2 * pair + 1, z)
             turned[s] = bank("turn%d" % (s % 2), [P, PASSES, 2, P])
             for u in range(2):
                 for c in range(PASSES):

from contextlib import ExitStack

import concourse.mybir as mybir
from concourse.masks import make_identity

K, N, T, S = 512, 512, 1024, 1024
FLOPS = 2 * K * N * (T + S)

F32 = mybir.dt.float32
BF16 = mybir.dt.bfloat16
I32 = mybir.dt.int32
U32 = mybir.dt.uint32
U8 = mybir.dt.uint8
E4M3 = mybir.dt.float8_e4m3fn_x4
E5M2 = mybir.dt.float8_e5m2_x4
E2M1 = mybir.dt.float4_e2m1fn_x4
ALU = mybir.AluOpType
COPY = mybir.ActivationFunctionType.Copy

P = 128
PASSES = 2
TILES = 4
OUT_SCALE = 0.03
VECTOR_SUM = 4
FIRST_STORED_STEP = 3


def tile_mix_covariances_of_two_stores_kernel(tc, xa, xb, ra, rb, sa_words, sa_scales, sb_words, sb_scales, out):
    nc = tc.nc
    steps = 2 * TILES
    last = steps - 1

    with ExitStack() as ctx:
        keep = ctx.enter_context(tc.tile_pool(name="keep", bufs=1))
        rows = ctx.enter_context(tc.tile_pool(name="rows", bufs=steps))
        psum = ctx.enter_context(tc.psum_pool(name="psum", bufs=1))
        ctx.enter_context(tc.manual_schedule())

        def bank(tag, shape):
            return psum.tile(shape, F32, name="bank", tag=tag)

        rb_cols = keep.tile([P, PASSES, 4], F32)
        ra_cols = keep.tile([P, PASSES, 4], F32)
        r_cols = (rb_cols, ra_cols)
        sa_codes = [keep.tile([P, 4 * K], U8, name="sa_codes%d" % z, align_bytes=64) for z in range(PASSES)]
        sb_codes = [keep.tile([P, 2 * N], U8, name="sb_codes%d" % z, align_bytes=64) for z in range(PASSES)]
        sa_plane = keep.tile([P, PASSES, K], U8, align_bytes=64)
        sb_plane = keep.tile([P, PASSES, N], U8, align_bytes=64)
        ident = keep.tile([P, P], F32)
        make_identity(nc, ident[:])
        nc.gpsimd.memset(sb_plane[:].bitcast(I32), 0)
        nc.gpsimd.memset(sa_plane[:].bitcast(I32), 0)
        x_rows = []

        def load_weights(engine, cols, r):
            engine.dma_start(out=cols[:], in_=r[0, :].rearrange("(c p j) -> p c j", c=PASSES, j=4))

        def load_rows(i, pieces=1):
            src = xb if i < TILES else xa
            x_tile = rows.tile([P, T], F32, name="x_tile")
            row0 = (i % TILES) * P
            width = T // pieces
            for t0 in range(0, T, width):
                nc.sync.dma_start(out=x_tile[:, t0 : t0 + width], in_=src[row0 : row0 + P, t0 : t0 + width])
            x_rows.append(x_tile)

        def load_scales(plane, scales):
            for q in range(4):
                nc.sync.dma_start(
                    out=plane[32 * q : 32 * q + 4, :, :].bitcast(I32),
                    in_=scales[:, 4 * q : 4 * q + 4, :].rearrange("z q c -> q z c").bitcast(I32),
                )

        def load_words(z):
            nc.sync.dma_start(out=sb_codes[z][:].bitcast(I32), in_=sb_words[z, :, :].bitcast(I32))
            nc.sync.dma_start(
                out=sa_codes[z][:].bitcast(I32), in_=sa_words[z, :, :, :].rearrange("p c r -> p (c r)").bitcast(I32)
            )

        load_weights(nc.scalar, rb_cols, rb)
        load_rows(0, pieces=2)
        load_rows(1)
        load_scales(sb_plane, sb_scales)
        load_rows(2)
        load_weights(nc.sync, ra_cols, ra)
        load_rows(3)
        load_scales(sa_plane, sa_scales)
        load_rows(4)
        load_words(0)
        load_rows(5)
        load_rows(6)
        load_words(1)
        load_rows(7)

        ta_codes = keep.tile([P, TILES * PASSES * P], U32, align_bytes=64)
        tb_codes = keep.tile([P, PASSES, N], U32, align_bytes=64)
        ta_plane = keep.tile([P, TILES * PASSES * P], U8, align_bytes=64)
        tb_plane = keep.tile([P, PASSES, N], U8, align_bytes=64)

        r_banks = {}
        neg_mean = {}
        centred = {}
        turned = {}
        grouped = {}
        acc = {}

        def spread_weights(which, u):
            tag = ("acc%d" % (2 + u)) if which == 0 else ("ra%d" % u)
            spread = bank(tag, [P, 2, PASSES, P])
            for e in range(2):
                for c in range(PASSES):
                    j = 2 * u + e
                    nc.tensor.transpose(
                        spread[:, e, c, :], r_cols[which][:, c, j : j + 1].to_broadcast([P, P]), ident[:]
                    )
            r_banks[which, u] = spread

        def scalar_mean(i, width):
            part = rows.tile([P, 1], F32, name="part")
            scaled = rows.tile([P, width], F32, name="scaled")
            nc.scalar.activation(out=scaled[:], in_=x_rows[i][:, :width], func=COPY, scale=-1.0 / T, accum_out=part[:])
            return part

        def vector_total(i, t0):
            half = (T - t0) // 2
            total = rows.tile([P, 1], F32, name="total", bufs=2)
            folded = rows.tile([P, half], F32, name="folded", bufs=2)
            nc.vector.scalar_tensor_tensor(
                out=folded[:], in0=x_rows[i][:, t0 : t0 + half], scalar=1.0, in1=x_rows[i][:, t0 + half :],
                op0=ALU.mult, op1=ALU.add, accum_out=total[:],
            )
            return total

        def vector_mean(total, rest):
            mean = rows.tile([P, 1], F32, name="mean", bufs=2)
            nc.vector.tensor_scalar(out=mean[:], in0=total[:], scalar1=-1.0 / T, scalar2=rest, op0=ALU.mult, op1=ALU.add)
            return mean

        def centre(i, u, passes):
            which = i // TILES
            pairs = slice(passes.start * P, passes.stop * P)
            x_pairs = x_rows[i][:].rearrange("p (n j) -> p n j", j=4)[:, pairs, 2 * u : 2 * u + 2]
            r_pairs = r_banks[which, u][:].rearrange("p e c n -> p (c n) e")[:, pairs, :]
            nc.vector.scalar_tensor_tensor(
                out=centred[i][:].rearrange("p (u n e) -> p u n e", u=2, e=2)[:, u, pairs, :],
                in0=x_pairs, scalar=neg_mean[i][:], in1=r_pairs, op0=ALU.add, op1=ALU.mult,
            )

        def turn(i, u, c, dst):
            words = centred[i][:].bitcast(F32)
            w0 = (u * PASSES + c) * P
            nc.tensor.transpose(dst, words[:, w0 : w0 + P], ident[:])

        def quantise_b(pair):
            cols = slice(pair * 2 * P, (pair + 1) * 2 * P)
            for c in range(PASSES):
                nc.vector.quantize_mx(
                    out=tb_codes[:, c, cols].bitcast(E5M2), scales=tb_plane[:, c, cols],
                    in_=grouped[2 * pair][:, c * 8 * P : (c + 1) * 8 * P],
                )

        def quantise_a(m, passes):
            cols = slice((m * PASSES + passes.start) * P, (m * PASSES + passes.stop) * P)
            nc.vector.quantize_mx(
                out=ta_codes[:, cols].bitcast(E4M3), scales=ta_plane[:, cols],
                in_=grouped[TILES + m][:, passes.start * 4 * P : passes.stop * 4 * P],
            )

        def stored_pass(m, z):
            if z == 0:
                acc[m] = bank("acc%d" % m, [P, N])
            nc.tensor.matmul_mx(
                out=acc[m][:],
                lhsT=sa_codes[z][:, 4 * P * m : 4 * P * (m + 1)].bitcast(E4M3),
                lhsT_scale=sa_plane[:, z, P * m : P * (m + 1)],
                rhs=sb_codes[z][:].bitcast(E2M1),
                rhs_scale=sb_plane[:, z, :],
                start=(z == 0), stop=False,
            )

        def fresh_pass(m, c):
            cols = slice((m * PASSES + c) * P, (m * PASSES + c + 1) * P)
            nc.tensor.matmul_mx(
                out=acc[m][:],
                lhsT=ta_codes[:, cols].bitcast(E4M3),
                lhsT_scale=ta_plane[:, cols],
                rhs=tb_codes[:, c, :].bitcast(E5M2),
                rhs_scale=tb_plane[:, c, :],
                start=False, stop=(c == PASSES - 1),
            )

        def store(m):
            result = rows.tile([P, N], F32, name="result", bufs=TILES - 1)
            nc.scalar.activation(out=result[:], in_=acc[m][:], func=COPY, scale=OUT_SCALE)
            nc.sync.dma_start(out=out[m * P : (m + 1) * P, :], in_=result[:])

        def store_last_half(h):
            m = TILES - 1
            cols = slice(h * (N // 2), (h + 1) * (N // 2))
            result_half = rows.tile([P, N // 2], F32, name="result_half", bufs=2)
            nc.vector.tensor_scalar(out=result_half[:], in0=acc[m][:, cols], scalar1=OUT_SCALE, scalar2=None, op0=ALU.mult)
            nc.sync.dma_start(out=out[m * P : (m + 1) * P, cols], in_=result_half[:])

        def copy_out(i):
            if i >= TILES:
                grouped[i] = rows.tile([P, T], BF16, name="grouped_a", bufs=TILES, align_bytes=64)
                dst = grouped[i][:].bitcast(F32).rearrange("p (c k u) -> p c k u", c=PASSES, u=2)
            else:
                if i % 2 == 0:
                    grouped[i] = rows.tile([P, 2 * T], BF16, name="grouped_b", bufs=2, align_bytes=64)
                both_tiles = grouped[i - i % 2][:].bitcast(F32).rearrange("p (c i k u) -> p c i k u", c=PASSES, i=2, u=2)
                dst = both_tiles[:, :, i % 2, :, :]
            nc.scalar.copy(out=dst, in_=turned[i][:].rearrange("p c u k -> p c k u"))

        both = range(0, PASSES)
        spread_weights(0, 0)
        spread_weights(0, 1)
        first_half = scalar_mean(0, T // 2)
        neg_mean[0] = vector_mean(vector_total(0, T // 2), first_half[:])
        neg_mean[1] = scalar_mean(1, T)
        for s in range(last):
            centred[s] = rows.tile([P, T], BF16, name="centred")
            if s + 1 == VECTOR_SUM:
                total = vector_total(s + 1, 0)
                centre(s, 0, both)
                neg_mean[s + 1] = vector_mean(total, 0.0)
                centre(s, 1, both)
            else:
                if s > 0:
                    neg_mean[s + 1] = scalar_mean(s + 1, T)
                centre(s, 0, both)
                centre(s, 1, both)
            if s > 0:
                copy_out(s - 1)
            if s >= FIRST_STORED_STEP:
                z, pair = divmod(s - FIRST_STORED_STEP, 2)
                stored_pass(2 * pair, z)
                stored_pass(2 * pair + 1, z)
            turned[s] = bank("turn%d" % (s % 2), [P, PASSES, 2, P])
            for u in range(2):
                for c in range(PASSES):
                    turn(s, u, c, turned[s][:, c, u, :])
            if s in (1, 2):
                spread_weights(1, s - 1)
            if s in (3, 5):
                quantise_b((s - 3) // 2)
            if s == 6:
                quantise_a(0, both)
                for c in range(PASSES):
                    fresh_pass(0, c)

        centred[last] = rows.tile([P, T], BF16, name="centred")
        grouped[last] = rows.tile([P, T], BF16, name="grouped_a", bufs=TILES, align_bytes=64)
        last_words = grouped[last][:].bitcast(F32).rearrange("p (c k u) -> p c k u", c=PASSES, u=2)

        def turn_last(c):
            half = bank("turn%d" % ((last + c) % 2), [P, 2, P])
            for u in range(2):
                turn(last, u, c, half[:, u, :])
            return half[:].rearrange("p u k -> p k u")

        for u in range(2):
            centre(last, u, range(0, 1))
        copy_out(last - 1)
        quantise_a(1, both)
        half0 = turn_last(0)
        for c in range(PASSES):
            fresh_pass(1, c)
        for u in range(2):
            centre(last, u, range(1, 2))
        store(0)
        quantise_a(2, both)
        half1 = turn_last(1)
        nc.scalar.copy(out=last_words[:, 0, :, :], in_=half0)
        for c in range(PASSES):
            fresh_pass(2, c)
        quantise_a(3, range(0, 1))
        fresh_pass(3, 0)
        nc.vector.tensor_copy(out=last_words[:, 1, :, :], in_=half1)
        store(1)
        quantise_a(3, range(1, 2))
        fresh_pass(3, 1)
        store(2)
        store_last_half(0)
        store_last_half(1)
